import numpy as np
import ml_dtypes

BF16 = ml_dtypes.bfloat16


def bf(x):
    return np.asarray(x, np.float32).astype(BF16)


def f32(x):
    return np.asarray(x, np.float32)


def f64(x):
    return np.asarray(x).astype(np.float64)


def striped(idx):
    return np.tile(idx.reshape(-1, 16).T, (8, 1))


S, K, M, N = 1024, 256, 512, 1024


def setup_inputs():
    return {"table": bf(np.random.standard_normal((K, S))), "w": bf(np.random.standard_normal((K, M)) / np.sqrt(K)), "b": f32(0.5 * np.random.standard_normal((M, 1))), "offs": striped(np.random.permutation(S))}


def reference(table, w, b, offs):
    idx = offs[:16].T.reshape(-1)
    x = f64(table)[:, idx]
    y = f64(w).T @ x
    return y + f64(b)

@@ -1,0 +1,49 @@
+import concourse.mybir as mybir
+
+BF16, F32, U16 = mybir.dt.bfloat16, mybir.dt.float32, mybir.dt.uint16
+
+P = 128
+K, S = 256, 1024
+M, N = 512, 1024
+PIECE = 512
+K_BLOCKS, M_BLOCKS, PIECES = K // P, M // P, N // PIECE
+PIECE_COLS = PIECE // 16
+
+FLOPS = 2 * K * M * N
+
+
+def tile_gather_matmul_kernel(tc, table, w, b, offs, out):
+    nc = tc.nc
+    with (
+        tc.tile_pool(name="held", bufs=1) as held,
+        tc.psum_pool(name="psum", bufs=1) as psum,
+    ):
+        offsets = held.tile([P, N // 16], U16, name="offsets")
+        nc.sync.dma_start(offsets[:], offs)
+
+        table_blocks = [held.tile([P, S], BF16, name=f"table{k}") for k in range(K_BLOCKS)]
+        w_blocks = [held.tile([P, M], BF16, name=f"w{k}") for k in range(K_BLOCKS)]
+        for k in range(K_BLOCKS):
+            nc.sync.dma_start(table_blocks[k][:], table[k * P : (k + 1) * P, :])
+            nc.scalar.dma_start(w_blocks[k][:], w[k * P : (k + 1) * P, :])
+
+        bias = held.tile([P, M_BLOCKS], F32, name="bias")
+        nc.scalar.dma_start(bias[:], b.rearrange("(a p) o -> p (a o)", p=P))
+
+        for m in range(M_BLOCKS):
+            for piece in range(PIECES):
+                picked = offsets[:, piece * PIECE_COLS : (piece + 1) * PIECE_COLS]
+                bank = psum.tile([P, PIECE], F32, name=f"bank{m}_{piece}")
+                for k in range(K_BLOCKS):
+                    nc.tensor.matmul(
+                        bank[:],
+                        w_blocks[k][:, m * P : (m + 1) * P],
+                        table_blocks[k][:].indirect(picked),
+                        start=(k == 0),
+                        stop=(k == K_BLOCKS - 1),
+                    )
+                y = held.tile([P, PIECE], F32, name=f"y{m}_{piece}")
+                nc.vector.tensor_scalar_add(y[:], bank[:], bias[:, m : m + 1])
+                nc.sync.dma_start(
+                    out[m * P : (m + 1) * P, piece * PIECE : (piece + 1) * PIECE], y[:]
+                )

@@ -8,6 +8,7 @@ M, N = 512, 1024
 PIECE = 512
 K_BLOCKS, M_BLOCKS, PIECES = K // P, M // P, N // PIECE
 PIECE_COLS = PIECE // 16
+WARM_UPS = 6
 
 FLOPS = 2 * K * M * N
 
@@ -30,10 +31,20 @@ def tile_gather_matmul_kernel(tc, table, w, b, offs, out):
         bias = held.tile([P, M_BLOCKS], F32, name="bias")
         nc.scalar.dma_start(bias[:], b.rearrange("(a p) o -> p (a o)", p=P))
 
+        banks = [
+            [psum.tile([P, PIECE], F32, name=f"bank{m}_{piece}") for piece in range(PIECES)]
+            for m in range(M_BLOCKS)
+        ]
+
+        zeros = held.tile([P, PIECE], BF16, name="zeros")
+        nc.vector.memset(zeros[:], 0.0)
+        for warm_up in range(WARM_UPS):
+            nc.tensor.matmul(banks[-1][-1][:], zeros[:, :P], zeros[:], start=True, stop=True)
+
         for m in range(M_BLOCKS):
             for piece in range(PIECES):
                 picked = offsets[:, piece * PIECE_COLS : (piece + 1) * PIECE_COLS]
-                bank = psum.tile([P, PIECE], F32, name=f"bank{m}_{piece}")
+                bank = banks[m][piece]
                 for k in range(K_BLOCKS):
                     nc.tensor.matmul(
                         bank[:],

@@ -8,7 +8,6 @@ M, N = 512, 1024
 PIECE = 512
 K_BLOCKS, M_BLOCKS, PIECES = K // P, M // P, N // PIECE
 PIECE_COLS = PIECE // 16
-WARM_UPS = 6
 
 FLOPS = 2 * K * M * N
 
@@ -20,41 +19,32 @@ def tile_gather_matmul_kernel(tc, table, w, b, offs, out):
         tc.psum_pool(name="psum", bufs=1) as psum,
     ):
         offsets = held.tile([P, N // 16], U16, name="offsets")
-        nc.sync.dma_start(offsets[:], offs)
-
         table_blocks = [held.tile([P, S], BF16, name=f"table{k}") for k in range(K_BLOCKS)]
         w_blocks = [held.tile([P, M], BF16, name=f"w{k}") for k in range(K_BLOCKS)]
-        for k in range(K_BLOCKS):
-            nc.sync.dma_start(table_blocks[k][:], table[k * P : (k + 1) * P, :])
-            nc.scalar.dma_start(w_blocks[k][:], w[k * P : (k + 1) * P, :])
-
         bias = held.tile([P, M_BLOCKS], F32, name="bias")
-        nc.scalar.dma_start(bias[:], b.rearrange("(a p) o -> p (a o)", p=P))
 
-        banks = [
-            [psum.tile([P, PIECE], F32, name=f"bank{m}_{piece}") for piece in range(PIECES)]
-            for m in range(M_BLOCKS)
-        ]
-
-        zeros = held.tile([P, PIECE], BF16, name="zeros")
-        nc.vector.memset(zeros[:], 0.0)
-        for warm_up in range(WARM_UPS):
-            nc.tensor.matmul(banks[-1][-1][:], zeros[:, :P], zeros[:], start=True, stop=True)
+        nc.sync.dma_start(offsets[:], offs)
+        for k in range(K_BLOCKS):
+            nc.sync.dma_start(w_blocks[k][:], w[k * P : (k + 1) * P, :])
+            nc.sync.dma_start(table_blocks[k][:], table[k * P : (k + 1) * P, :])
+        nc.sync.dma_start(bias[:], b.rearrange("(a p) o -> p (a o)", p=P))
 
         for m in range(M_BLOCKS):
-            for piece in range(PIECES):
-                picked = offsets[:, piece * PIECE_COLS : (piece + 1) * PIECE_COLS]
-                bank = banks[m][piece]
-                for k in range(K_BLOCKS):
+            banks = [psum.tile([P, PIECE], F32, name=f"bank{m}_{piece}") for piece in range(PIECES)]
+            for k in range(K_BLOCKS):
+                for piece in range(PIECES):
                     nc.tensor.matmul(
-                        bank[:],
+                        banks[piece][:],
                         w_blocks[k][:, m * P : (m + 1) * P],
-                        table_blocks[k][:].indirect(picked),
+                        table_blocks[k][:].indirect(
+                            offsets[:, piece * PIECE_COLS : (piece + 1) * PIECE_COLS]
+                        ),
                         start=(k == 0),
                         stop=(k == K_BLOCKS - 1),
                     )
+            for piece in range(PIECES):
                 y = held.tile([P, PIECE], F32, name=f"y{m}_{piece}")
-                nc.vector.tensor_scalar_add(y[:], bank[:], bias[:, m : m + 1])
+                nc.vector.tensor_scalar_add(y[:], banks[piece][:], bias[:, m : m + 1])
                 nc.sync.dma_start(
                     out[m * P : (m + 1) * P, piece * PIECE : (piece + 1) * PIECE], y[:]
                 )

@@ -24,9 +24,11 @@ def tile_gather_matmul_kernel(tc, table, w, b, offs, out):
         bias = held.tile([P, M_BLOCKS], F32, name="bias")
 
         nc.sync.dma_start(offsets[:], offs)
-        for k in range(K_BLOCKS):
-            nc.sync.dma_start(w_blocks[k][:], w[k * P : (k + 1) * P, :])
-            nc.sync.dma_start(table_blocks[k][:], table[k * P : (k + 1) * P, :])
+        nc.sync.dma_start(w_blocks[0][:, 0:P], w[0:P, 0:P])
+        nc.sync.dma_start(table_blocks[0][:], table[0:P, :])
+        nc.sync.dma_start(w_blocks[1][:], w[P : 2 * P, :])
+        nc.sync.dma_start(table_blocks[1][:], table[P : 2 * P, :])
+        nc.sync.dma_start(w_blocks[0][:, P:M], w[0:P, P:M])
         nc.sync.dma_start(bias[:], b.rearrange("(a p) o -> p (a o)", p=P))
 
         for m in range(M_BLOCKS):

@@ -44,9 +44,14 @@ def tile_gather_matmul_kernel(tc, table, w, b, offs, out):
                         start=(k == 0),
                         stop=(k == K_BLOCKS - 1),
                     )
+            y = held.tile([P, N], F32, name=f"y{m}")
             for piece in range(PIECES):
-                y = held.tile([P, PIECE], F32, name=f"y{m}_{piece}")
-                nc.vector.tensor_scalar_add(y[:], banks[piece][:], bias[:, m : m + 1])
-                nc.sync.dma_start(
-                    out[m * P : (m + 1) * P, piece * PIECE : (piece + 1) * PIECE], y[:]
+                nc.vector.tensor_scalar_add(
+                    y[:, piece * PIECE : (piece + 1) * PIECE], banks[piece][:], bias[:, m : m + 1]
                 )
+            if m < M_BLOCKS - 1:
+                nc.sync.dma_start(out[m * P : (m + 1) * P, :], y[:])
+            else:
+                for piece in range(PIECES):
+                    columns = slice(piece * PIECE, (piece + 1) * PIECE)
+                    nc.sync.dma_start(out[m * P : (m + 1) * P, columns], y[:, columns])

@@ -33,25 +33,29 @@ def tile_gather_matmul_kernel(tc, table, w, b, offs, out):
 
         for m in range(M_BLOCKS):
             banks = [psum.tile([P, PIECE], F32, name=f"bank{m}_{piece}") for piece in range(PIECES)]
-            for k in range(K_BLOCKS):
-                for piece in range(PIECES):
-                    nc.tensor.matmul(
-                        banks[piece][:],
-                        w_blocks[k][:, m * P : (m + 1) * P],
-                        table_blocks[k][:].indirect(
-                            offsets[:, piece * PIECE_COLS : (piece + 1) * PIECE_COLS]
-                        ),
-                        start=(k == 0),
-                        stop=(k == K_BLOCKS - 1),
-                    )
-            y = held.tile([P, N], F32, name=f"y{m}")
-            for piece in range(PIECES):
-                nc.vector.tensor_scalar_add(
-                    y[:, piece * PIECE : (piece + 1) * PIECE], banks[piece][:], bias[:, m : m + 1]
+            if m == 0:
+                steps = [(k, piece) for k in range(K_BLOCKS) for piece in range(PIECES)]
+            else:
+                steps = [(k, piece) for piece in range(PIECES) for k in range(K_BLOCKS)]
+            for k, piece in steps:
+                nc.tensor.matmul(
+                    banks[piece][:],
+                    w_blocks[k][:, m * P : (m + 1) * P],
+                    table_blocks[k][:].indirect(
+                        offsets[:, piece * PIECE_COLS : (piece + 1) * PIECE_COLS]
+                    ),
+                    start=(k == 0),
+                    stop=(k == K_BLOCKS - 1),
                 )
             if m < M_BLOCKS - 1:
-                nc.sync.dma_start(out[m * P : (m + 1) * P, :], y[:])
+                add_cuts, store_cuts = [0, PIECE, N], [0, N]
             else:
-                for piece in range(PIECES):
-                    columns = slice(piece * PIECE, (piece + 1) * PIECE)
-                    nc.sync.dma_start(out[m * P : (m + 1) * P, columns], y[:, columns])
+                add_cuts = store_cuts = [0, PIECE, PIECE + PIECE // 2, N]
+            y = held.tile([P, N], F32, name=f"y{m}")
+            for lo, hi in zip(add_cuts, add_cuts[1:]):
+                bank_columns = slice(lo % PIECE, lo % PIECE + hi - lo)
+                nc.vector.tensor_scalar_add(
+                    y[:, lo:hi], banks[lo // PIECE][:, bank_columns], bias[:, m : m + 1]
+                )
+            for lo, hi in zip(store_cuts, store_cuts[1:]):
+                nc.sync.dma_start(out[m * P : (m + 1) * P, lo:hi], y[:, lo:hi])

@@ -47,8 +47,10 @@ def tile_gather_matmul_kernel(tc, table, w, b, offs, out):
                     start=(k == 0),
                     stop=(k == K_BLOCKS - 1),
                 )
-            if m < M_BLOCKS - 1:
+            if m < M_BLOCKS // 2:
                 add_cuts, store_cuts = [0, PIECE, N], [0, N]
+            elif m < M_BLOCKS - 1:
+                add_cuts = store_cuts = [0, PIECE, N]
             else:
                 add_cuts = store_cuts = [0, PIECE, PIECE + PIECE // 2, N]
             y = held.tile([P, N], F32, name=f"y{m}")

@@ -23,9 +23,9 @@ def tile_gather_matmul_kernel(tc, table, w, b, offs, out):
         w_blocks = [held.tile([P, M], BF16, name=f"w{k}") for k in range(K_BLOCKS)]
         bias = held.tile([P, M_BLOCKS], F32, name="bias")
 
+        nc.sync.dma_start(table_blocks[0][:], table[0:P, :])
         nc.sync.dma_start(offsets[:], offs)
         nc.sync.dma_start(w_blocks[0][:, 0:P], w[0:P, 0:P])
-        nc.sync.dma_start(table_blocks[0][:], table[0:P, :])
         nc.sync.dma_start(w_blocks[1][:], w[P : 2 * P, :])
         nc.sync.dma_start(table_blocks[1][:], table[P : 2 * P, :])
         nc.sync.dma_start(w_blocks[0][:, P:M], w[0:P, P:M])

@@ -47,17 +47,14 @@ def tile_gather_matmul_kernel(tc, table, w, b, offs, out):
                     start=(k == 0),
                     stop=(k == K_BLOCKS - 1),
                 )
-            if m < M_BLOCKS // 2:
-                add_cuts, store_cuts = [0, PIECE, N], [0, N]
-            elif m < M_BLOCKS - 1:
-                add_cuts = store_cuts = [0, PIECE, N]
+            if m < M_BLOCKS - 1:
+                cuts = [0, PIECE, N]
             else:
-                add_cuts = store_cuts = [0, PIECE, PIECE + PIECE // 2, N]
+                cuts = [0, PIECE, PIECE + PIECE // 2, N]
             y = held.tile([P, N], F32, name=f"y{m}")
-            for lo, hi in zip(add_cuts, add_cuts[1:]):
+            for lo, hi in zip(cuts, cuts[1:]):
                 bank_columns = slice(lo % PIECE, lo % PIECE + hi - lo)
                 nc.vector.tensor_scalar_add(
                     y[:, lo:hi], banks[lo // PIECE][:, bank_columns], bias[:, m : m + 1]
                 )
-            for lo, hi in zip(store_cuts, store_cuts[1:]):
                 nc.sync.dma_start(out[m * P : (m + 1) * P, lo:hi], y[:, lo:hi])

@@ -8,6 +8,7 @@ M, N = 512, 1024
 PIECE = 512
 K_BLOCKS, M_BLOCKS, PIECES = K // P, M // P, N // PIECE
 PIECE_COLS = PIECE // 16
+BURST = 256
 
 FLOPS = 2 * K * M * N
 
@@ -18,10 +19,14 @@ def tile_gather_matmul_kernel(tc, table, w, b, offs, out):
         tc.tile_pool(name="held", bufs=1) as held,
         tc.psum_pool(name="psum", bufs=1) as psum,
     ):
-        offsets = held.tile([P, N // 16], U16, name="offsets")
-        table_blocks = [held.tile([P, S], BF16, name=f"table{k}") for k in range(K_BLOCKS)]
-        w_blocks = [held.tile([P, M], BF16, name=f"w{k}") for k in range(K_BLOCKS)]
-        bias = held.tile([P, M_BLOCKS], F32, name="bias")
+        offsets = held.tile([P, N // 16], U16, name="offsets", align_bytes=BURST)
+        table_blocks = [
+            held.tile([P, S], BF16, name=f"table{k}", align_bytes=BURST) for k in range(K_BLOCKS)
+        ]
+        w_blocks = [
+            held.tile([P, M], BF16, name=f"w{k}", align_bytes=BURST) for k in range(K_BLOCKS)
+        ]
+        bias = held.tile([P, M_BLOCKS], F32, name="bias", align_bytes=BURST)
 
         nc.sync.dma_start(table_blocks[0][:], table[0:P, :])
         nc.sync.dma_start(offsets[:], offs)
@@ -51,7 +56,7 @@ def tile_gather_matmul_kernel(tc, table, w, b, offs, out):
                 cuts = [0, PIECE, N]
             else:
                 cuts = [0, PIECE, PIECE + PIECE // 2, N]
-            y = held.tile([P, N], F32, name=f"y{m}")
+            y = held.tile([P, N], F32, name=f"y{m}", align_bytes=BURST)
             for lo, hi in zip(cuts, cuts[1:]):
                 bank_columns = slice(lo % PIECE, lo % PIECE + hi - lo)
                 nc.vector.tensor_scalar_add(

import concourse.mybir as mybir

BF16, F32, U16 = mybir.dt.bfloat16, mybir.dt.float32, mybir.dt.uint16

P = 128
K, S = 256, 1024
M, N = 512, 1024
PIECE = 512
K_BLOCKS, M_BLOCKS, PIECES = K // P, M // P, N // PIECE
PIECE_COLS = PIECE // 16
BURST = 256

FLOPS = 2 * K * M * N


def tile_gather_matmul_kernel(tc, table, w, b, offs, out):
    nc = tc.nc
    with (
        tc.tile_pool(name="held", bufs=1) as held,
        tc.psum_pool(name="psum", bufs=1) as psum,
    ):
        offsets = held.tile([P, N // 16], U16, name="offsets", align_bytes=BURST)
        table_blocks = [
            held.tile([P, S], BF16, name=f"table{k}", align_bytes=BURST) for k in range(K_BLOCKS)
        ]
        w_blocks = [
            held.tile([P, M], BF16, name=f"w{k}", align_bytes=BURST) for k in range(K_BLOCKS)
        ]
        bias = held.tile([P, M_BLOCKS], F32, name="bias", align_bytes=BURST)

        nc.sync.dma_start(table_blocks[0][:], table[0:P, :])
        nc.sync.dma_start(offsets[:], offs)
        nc.sync.dma_start(w_blocks[0][:, 0:P], w[0:P, 0:P])
        nc.sync.dma_start(w_blocks[1][:], w[P : 2 * P, :])
        nc.sync.dma_start(table_blocks[1][:], table[P : 2 * P, :])
        nc.sync.dma_start(w_blocks[0][:, P:M], w[0:P, P:M])
        nc.sync.dma_start(bias[:], b.rearrange("(a p) o -> p (a o)", p=P))

        for m in range(M_BLOCKS):
            banks = [psum.tile([P, PIECE], F32, name=f"bank{m}_{piece}") for piece in range(PIECES)]
            if m == 0:
                steps = [(k, piece) for k in range(K_BLOCKS) for piece in range(PIECES)]
            else:
                steps = [(k, piece) for piece in range(PIECES) for k in range(K_BLOCKS)]
            for k, piece in steps:
                nc.tensor.matmul(
                    banks[piece][:],
                    w_blocks[k][:, m * P : (m + 1) * P],
                    table_blocks[k][:].indirect(
                        offsets[:, piece * PIECE_COLS : (piece + 1) * PIECE_COLS]
                    ),
                    start=(k == 0),
                    stop=(k == K_BLOCKS - 1),
                )
            if m < M_BLOCKS - 1:
                cuts = [0, PIECE, N]
            else:
                cuts = [0, PIECE, PIECE + PIECE // 2, N]
            y = held.tile([P, N], F32, name=f"y{m}", align_bytes=BURST)
            for lo, hi in zip(cuts, cuts[1:]):
                bank_columns = slice(lo % PIECE, lo % PIECE + hi - lo)
                nc.vector.tensor_scalar_add(
                    y[:, lo:hi], banks[lo // PIECE][:, bank_columns], bias[:, m : m + 1]
                )
                nc.sync.dma_start(out[m * P : (m + 1) * P, lo:hi], y[:, lo:hi])
